import numpy as np
import ml_dtypes


def mxq(x, axis, fmt="e4m3"):
    dtype, down = {"e4m3": (ml_dtypes.float8_e4m3fn, 7), "e5m2": (ml_dtypes.float8_e5m2, 14)}[fmt]
    v = np.moveaxis(np.asarray(x, np.float32).astype(ml_dtypes.bfloat16).astype(np.float64), axis, -1)
    blocks = v.reshape(v.shape[:-1] + (-1, 32))
    amax = np.abs(blocks).max(-1, keepdims=True)
    byte = np.maximum(np.where(amax > 0, np.frexp(amax)[1] - 1 + 127, 0) - down, 1)
    scale = np.exp2(byte - 127.0)
    codes = (blocks / scale).astype(np.float32).astype(dtype).astype(np.float64)
    return np.moveaxis((codes * scale).reshape(v.shape), -1, axis)


WIDE = False


def mx_kscale(k):
    if not WIDE:
        return np.ones(k)
    levels = np.array([10, -10, 5, -5, 0])
    if k % 512:
        return np.exp2(np.random.permutation(np.resize(levels, k // 32))).repeat(32)
    a = np.empty((k // 512, 16))
    for p in range(k // 512):
        a[p, :8] = np.random.permutation(np.resize(levels, 8))
        for g in range(8):
            far = levels[np.abs(levels - a[p, g]) >= 10]
            a[p, g + 8] = far[np.random.randint(len(far))]
    return np.exp2(a.ravel()).repeat(32)


def f64(x):
    return np.asarray(x).astype(np.float64)


def striped(idx):
    return np.tile(idx.reshape(-1, 16).T, (8, 1)).astype(np.uint16)


def unstriped(offs):
    return offs[:16].T.reshape(-1).astype(np.int64)


def striped8(idx):
    return np.concatenate([x.reshape(-1, 16).T for x in idx]).astype(np.uint16)


def runs(offs, k):
    lists = np.stack([offs[16 * r : 16 * r + 16].T.reshape(-1) for r in range(8)]).astype(np.int64)
    return lists[np.arange(k) % 512 // 64]


def pack_weight(w):
    k, n = w.shape
    w = f64(np.asarray(w, np.float32).astype(ml_dtypes.bfloat16)).reshape(k // 32, 32, n)
    amax = np.abs(w).max(1)
    byte = np.clip(np.where(amax > 0, np.frexp(amax)[1] - 1 + 127 - 7, 1), 1, 254)
    scaled = (w * np.exp2(127.0 - byte)[:, None, :]).reshape(k, n).astype(np.float32)
    words = np.ascontiguousarray(scaled.reshape(k // 512, 128, 4, n).transpose(0, 1, 3, 2)).astype(ml_dtypes.float8_e4m3fn).view(np.uint8)
    return words, np.ascontiguousarray(byte.astype(np.uint8).reshape(k // 512, 16, n))


def unpack_weight(words, scales):
    g, p, n, _ = words.shape
    vals = np.ascontiguousarray(words).view(ml_dtypes.float8_e4m3fn).astype(np.float64) * np.repeat(np.exp2(scales.astype(np.float64) - 127.0), 8, axis=1)[..., None]
    return vals.transpose(0, 1, 3, 2).reshape(g * 512, n)


K, T, S, H, J = 512, 2048, 512, 512, 512


def setup_inputs():
    n = np.random.standard_normal
    s = mx_kscale(K)[:, None]
    u = mx_kscale(H)
    packed_xT = pack_weight(n((K, T)) * s)
    return {
        "x_words": packed_xT[0],
        "x_scales": packed_xT[1],
        "w1": (n((K, H)) / np.sqrt(K) / s).astype(np.float32),
        "tab": n((H, J)).astype(np.float32),
        "tab2": np.random.uniform(0.4, 1.4, (H, J)).astype(np.float32),
        "gn": (np.random.uniform(0.5, 1.5, (H, 1)) * u[:, None]).astype(np.float32),
        "w2": (n((H, H)) / np.sqrt(H) / u[:, None]).astype(np.float32),
        "offs": striped(np.random.permutation(T)[:S]),
        "n1": striped8(np.random.randint(0, J, (8, S))),
        "n2": striped8(np.stack([np.random.permutation(S) for _ in range(8)])),
        "n3": striped8(np.random.randint(0, J, (8, S))),
        "n4": striped8(np.stack([np.random.permutation(S) for _ in range(8)])),
        "n5": striped8(np.stack([np.random.permutation(S) for _ in range(8)])),
        "n6": striped8(np.stack([np.random.permutation(S) for _ in range(8)])),
        "n7": striped8(np.stack([np.random.permutation(S) for _ in range(8)])),
        "n8": striped8(np.stack([np.random.permutation(S) for _ in range(8)])),
    }


def reference(x_words, x_scales, w1, tab, tab2, gn, w2, offs, n1, n2, n3, n4, n5, n6, n7, n8):
    xq = unpack_weight(x_words, x_scales)[:, unstriped(offs)]
    y = mxq(f64(w1), 0, "e4m3").T @ xq
    z = f64(gn) * (np.abs(y - (y[np.arange(H)[:, None], runs(n2, H)]) - (f64(tab)[np.arange(H)[:, None], runs(n1, H)])))
    w2q = mxq(f64(w2), 0, "e4m3")
    a = w2q.T @ mxq(z, 0, "e4m3")
    z2 = f64(gn) * (y * (f64(tab2)[np.arange(H)[:, None], runs(n3, H)]) - (0.5 * (y[np.arange(H)[:, None], runs(n4, H)])))
    b = w2q.T @ mxq(z2, 0, "e4m3")
    return np.maximum(a[np.arange(H)[:, None], runs(n5, H)] + b[np.arange(H)[:, None], runs(n7, H)], a[np.arange(H)[:, None], runs(n6, H)] + b[np.arange(H)[:, None], runs(n8, H)])

@@ -1,0 +1,195 @@
+from contextlib import ExitStack
+
+import concourse.mybir as mybir
+
+F32 = mybir.dt.float32
+BF16 = mybir.dt.bfloat16
+I32 = mybir.dt.int32
+U32 = mybir.dt.uint32
+U16 = mybir.dt.uint16
+U8 = mybir.dt.uint8
+FP8X4 = mybir.dt.float8_e4m3fn_x4
+ALU = mybir.AluOpType
+ACT = mybir.ActivationFunctionType
+
+P = 128
+PACK = 4
+T = 2048
+S = 512
+H = 512
+FLOPS = 3 * 2 * 512 * 512 * 512
+
+
+def tile_picked_tiepathbkinddkindg_none_p_kernel(tc, x_words, x_scales, w1, tab, tab2, gn, w2, offs, n1, n2, n3, n4, n5, n6, n7, n8, out):
+    nc = tc.nc
+    with ExitStack() as ctx:
+        lists = ctx.enter_context(tc.tile_pool(name="lists", bufs=1))
+        keep = ctx.enter_context(tc.tile_pool(name="keep", bufs=1))
+        psum = ctx.enter_context(tc.psum_pool(name="psum", bufs=1))
+
+        def load_list(src, name):
+            tile = lists.tile([P, S // 16], U16, name=name)
+            nc.sync.dma_start(tile[:], src)
+            return tile
+
+        def planes(name, dtype, width):
+            return [keep.tile([P, width], dtype, name="%s%d" % (name, t), align_bytes=64) for t in range(PACK)]
+
+        def mx_pair(name, width):
+            codes = keep.tile([P, width], U32, name=name + "_codes", align_bytes=64)
+            scales = keep.tile([P, width], U8, name=name + "_scales", align_bytes=64)
+            return codes, scales
+
+        def quantize(pair, src, lo, hi):
+            nc.vector.quantize_mx(out=pair[0][:, lo:hi].bitcast(FP8X4), scales=pair[1][:, lo:hi], in_=src[:, PACK * lo : PACK * hi])
+
+        def product(bank, w_pair, t, x_pair):
+            cols = slice(t * P, (t + 1) * P)
+            nc.tensor.matmul_mx(out=bank[:], lhsT=w_pair[0][:, cols].bitcast(FP8X4), lhsT_scale=w_pair[1][:, cols],
+                                rhs=x_pair[0][:].bitcast(FP8X4), rhs_scale=x_pair[1][:], start=True, stop=True)
+
+        def by_row(src):
+            return src.rearrange("(p t) c -> p t c", t=PACK)
+
+        xw = keep.tile([P, T], I32, name="xw", align_bytes=64)
+        xs = keep.tile([P, T], U8, name="xs", align_bytes=64)
+        nc.vector.memset(xs[:].bitcast(I32), 0)
+        nc.sync.dma_start(xw[:], x_words[0].rearrange("p n r -> p (n r)").bitcast(I32))
+        l0 = load_list(offs, "l0")
+        for q in range(4):
+            nc.sync.dma_start(xs[32 * q : 32 * q + 4, :].bitcast(I32), x_scales[0, 4 * q : 4 * q + 4, :].bitcast(I32))
+        half = H // 2
+        w1_raw = [keep.tile([P, PACK, half], F32, name="w1_raw%d" % h, align_bytes=64) for h in range(2)]
+        for h in range(2):
+            nc.sync.dma_start(w1_raw[h][:], by_row(w1)[:, :, h * half : (h + 1) * half])
+        gain = keep.tile([P, PACK], F32, name="gain")
+        nc.sync.dma_start(gain[:], gn.rearrange("(p t) o -> p (t o)", t=PACK))
+        tab_win = planes("tab_win", F32, 2 * S)
+        tab2_win = planes("tab2_win", F32, 2 * S)
+        y_win = planes("y_win", F32, 2 * S)
+        nc.sync.dma_start(tab_win[0][:, S:], by_row(tab)[:, 0, :])
+        l1 = load_list(n1, "l1")
+        l2 = load_list(n2, "l2")
+        for t in range(1, PACK):
+            nc.sync.dma_start(tab_win[t][:, S:], by_row(tab)[:, t, :])
+        w2_raw = keep.tile([P, PACK, H], F32, name="w2_raw", align_bytes=64)
+        nc.sync.dma_start(w2_raw[:], by_row(w2))
+        l3 = load_list(n3, "l3")
+        l4 = load_list(n4, "l4")
+        for t in range(PACK):
+            nc.sync.dma_start(tab2_win[t][:, :S], by_row(tab2)[:, t, :])
+        l5 = load_list(n5, "l5")
+        l6 = load_list(n6, "l6")
+        l7 = load_list(n7, "l7")
+        l8 = load_list(n8, "l8")
+
+        x_pair = mx_pair("x", S)
+        nc.vector.tensor_copy(x_pair[0][:], xw[:].bitcast(U32).indirect(l0[:]))
+        nc.vector.tensor_copy(x_pair[1][:], xs[:].indirect(l0[:]))
+
+        def dealt(dst, lo, hi):
+            return dst[:].rearrange("p (t m j) -> p m t j", t=PACK, j=PACK)[:, lo:hi]
+
+        def dealing(src):
+            return src.rearrange("p j (m t) -> p m t j", t=PACK)
+
+        w1_bf = keep.tile([P, PACK * H], BF16, name="w1_bf", align_bytes=64)
+        nc.scalar.copy(dealt(w1_bf, 0, P // 2), dealing(w1_raw[0][:]))
+        nc.vector.tensor_copy(dealt(w1_bf, P // 2, P), dealing(w1_raw[1][:]))
+        w1_pair = mx_pair("w1", H)
+        for h in range(2):
+            quantize(w1_pair, w1_bf, h * half, (h + 1) * half)
+
+        size = keep.tile([P, PACK], F32, name="size")
+        size2 = keep.tile([P, PACK], F32, name="size2")
+        step = keep.tile([P, PACK], F32, name="step")
+        sgn = keep.tile([P, PACK], F32, name="sgn")
+        nc.scalar.activation(size[:], gain[:], ACT.Abs)
+        nc.scalar.activation(size2[:], gain[:], ACT.Abs, scale=2.0)
+        nc.gpsimd.tensor_scalar(step[:], gain[:], 0.0, 2.0, ALU.is_ge, ALU.mult)
+        nc.gpsimd.tensor_scalar(sgn[:], step[:], 1.0, -1.0, ALU.mult, ALU.add)
+
+        for t in range(PACK):
+            bank = psum.tile([P, S], F32, name="first%d" % t)
+            product(bank, w1_pair, t, x_pair)
+            nc.scalar.activation(tab_win[t][:, :S], tab_win[t][:, S:], ACT.Copy, scale=size[:, t : t + 1])
+            nc.scalar.activation(y_win[t][:, :S], bank[:], ACT.Copy, scale=size[:, t : t + 1])
+            nc.scalar.activation(y_win[t][:, S:], bank[:], ACT.Copy, scale=size2[:, t : t + 1])
+
+        s4 = keep.tile([P, PACK, S], F32, name="s4", align_bytes=64)
+        q4 = keep.tile([P, PACK, S], F32, name="q4", align_bytes=64)
+        prod = planes("prod", F32, S)
+
+        def g1(t):
+            nc.vector.tensor_tensor(tab2_win[t][:, S:], tab_win[t][:].indirect(l1[:]), y_win[t][:, :S], ALU.subtract)
+
+        def g2(t):
+            nc.vector.tensor_tensor(s4[:, t, :], y_win[t][:].indirect(l2[:]), tab2_win[t][:, S:], ALU.add)
+
+        def g3(t):
+            nc.vector.tensor_tensor(prod[t][:], tab2_win[t][:].indirect(l3[:]), y_win[t][:, S:], ALU.mult)
+
+        def g4(t):
+            nc.vector.tensor_tensor(q4[:, t, :], y_win[t][:].indirect(l4[:]), prod[t][:], ALU.subtract)
+
+        def skewed(first, second):
+            first(0)
+            for t in range(1, PACK):
+                first(t)
+                second(t - 1)
+            second(PACK - 1)
+
+        def weave(dst, src, func, scale):
+            nc.scalar.activation(dst[:].rearrange("p (c i t) -> p c t i", i=4, t=PACK), src[:].rearrange("p t (c i) -> p c t i", i=4), func, scale=scale)
+
+        skewed(g1, g2)
+
+        w2_signed = keep.tile([P, PACK, H], BF16, name="w2_signed", align_bytes=64)
+        for j in range(PACK):
+            nc.scalar.activation(w2_signed[:, j, :], w2_raw[:, j, :], ACT.Copy, scale=sgn[:, j : j + 1])
+        w2_bf = keep.tile([P, PACK * H], BF16, name="w2_bf", align_bytes=64)
+        nc.scalar.copy(dealt(w2_bf, 0, P), dealing(w2_signed[:]))
+        w2_pair = mx_pair("w2", H)
+        quantize(w2_pair, w2_bf, 0, H)
+
+        z_bf = keep.tile([P, PACK * S], BF16, name="z_bf", align_bytes=64)
+        weave(z_bf, s4, ACT.Abs, 1.0)
+        for t in range(PACK):
+            g3(t)
+        z_pair = mx_pair("z", S)
+        quantize(z_pair, z_bf, 0, S)
+        for t in range(PACK):
+            bank = psum.tile([P, S], F32, name="second%d" % t)
+            product(bank, w2_pair, t, z_pair)
+            nc.scalar.copy(tab_win[t][:, :S], bank[:])
+        for t in range(PACK):
+            g4(t)
+        z2_bf = keep.tile([P, PACK * S], BF16, name="z2_bf", align_bytes=64)
+        weave(z2_bf, q4, ACT.Copy, -0.5)
+
+        a5 = planes("a5_", F32, S)
+        a6 = planes("a6_", F32, S)
+        for t in range(PACK):
+            nc.vector.tensor_copy(a5[t][:], tab_win[t][:].indirect(l5[:]))
+        z2_pair = mx_pair("z2", S)
+        quantize(z2_pair, z2_bf, 0, S)
+        for t in range(PACK):
+            bank = psum.tile([P, S], F32, name="first%d" % t)
+            product(bank, w2_pair, t, z2_pair)
+            nc.scalar.copy(tab2_win[t][:, :S], bank[:])
+        for t in range(PACK):
+            nc.vector.tensor_copy(a6[t][:], tab_win[t][:].indirect(l6[:]))
+
+        left = planes("left", F32, S)
+        right = planes("right", F32, S)
+        best = planes("best", F32, S)
+
+        def sums(t):
+            nc.vector.tensor_tensor(left[t][:], tab2_win[t][:].indirect(l7[:]), a5[t][:], ALU.add)
+            nc.vector.tensor_tensor(right[t][:], tab2_win[t][:].indirect(l8[:]), a6[t][:], ALU.add)
+
+        def larger(t):
+            nc.vector.tensor_tensor(best[t][:], left[t][:], right[t][:], ALU.max)
+            nc.sync.dma_start(by_row(out)[:, t, :], best[t][:])
+
+        skewed(sums, larger)

@@ -1,6 +1,7 @@
 from contextlib import ExitStack
 
 import concourse.mybir as mybir
+from concourse.masks import make_identity
 
 F32 = mybir.dt.float32
 BF16 = mybir.dt.bfloat16
@@ -51,37 +52,49 @@ def tile_picked_tiepathbkinddkindg_none_p_kernel(tc, x_words, x_scales, w1, tab,
         def by_row(src):
             return src.rearrange("(p t) c -> p t c", t=PACK)
 
+        tab_win = planes("tab_win", F32, 2 * S)
+        tab2_win = planes("tab2_win", F32, 2 * S)
+        y_win = planes("y_win", F32, 2 * S)
         xw = keep.tile([P, T], I32, name="xw", align_bytes=64)
         xs = keep.tile([P, T], U8, name="xs", align_bytes=64)
         nc.vector.memset(xs[:].bitcast(I32), 0)
+        l1 = load_list(n1, "l1")
+        for t in range(2):
+            nc.sync.dma_start(tab_win[t][:, :S], by_row(tab)[:, t, :])
+        gain = keep.tile([P, PACK], F32, name="gain")
+        nc.sync.dma_start(gain[:], gn.rearrange("(p t) o -> p (t o)", t=PACK))
+        nc.sync.dma_start(tab_win[2][:, :S], by_row(tab)[:, 2, :])
         nc.sync.dma_start(xw[:], x_words[0].rearrange("p n r -> p (n r)").bitcast(I32))
-        l0 = load_list(offs, "l0")
         for q in range(4):
             nc.sync.dma_start(xs[32 * q : 32 * q + 4, :].bitcast(I32), x_scales[0, 4 * q : 4 * q + 4, :].bitcast(I32))
+        l0 = load_list(offs, "l0")
         half = H // 2
         w1_raw = [keep.tile([P, PACK, half], F32, name="w1_raw%d" % h, align_bytes=64) for h in range(2)]
         for h in range(2):
             nc.sync.dma_start(w1_raw[h][:], by_row(w1)[:, :, h * half : (h + 1) * half])
-        gain = keep.tile([P, PACK], F32, name="gain")
-        nc.sync.dma_start(gain[:], gn.rearrange("(p t) o -> p (t o)", t=PACK))
-        tab_win = planes("tab_win", F32, 2 * S)
-        tab2_win = planes("tab2_win", F32, 2 * S)
-        y_win = planes("y_win", F32, 2 * S)
-        nc.sync.dma_start(tab_win[0][:, S:], by_row(tab)[:, 0, :])
-        l1 = load_list(n1, "l1")
-        l2 = load_list(n2, "l2")
-        for t in range(1, PACK):
-            nc.sync.dma_start(tab_win[t][:, S:], by_row(tab)[:, t, :])
-        w2_raw = keep.tile([P, PACK, H], F32, name="w2_raw", align_bytes=64)
-        nc.sync.dma_start(w2_raw[:], by_row(w2))
+        nc.sync.dma_start(tab_win[3][:, :S], by_row(tab)[:, 3, :])
         l3 = load_list(n3, "l3")
         l4 = load_list(n4, "l4")
         for t in range(PACK):
             nc.sync.dma_start(tab2_win[t][:, :S], by_row(tab2)[:, t, :])
-        l5 = load_list(n5, "l5")
-        l6 = load_list(n6, "l6")
+        w2_raw = keep.tile([P, PACK, H], F32, name="w2_raw", align_bytes=64)
+        nc.sync.dma_start(w2_raw[:], by_row(w2))
+        l2 = load_list(n2, "l2")
         l7 = load_list(n7, "l7")
         l8 = load_list(n8, "l8")
+        l5 = load_list(n5, "l5")
+        l6 = load_list(n6, "l6")
+
+        ident = keep.tile([P, P], F32, name="ident")
+        make_identity(nc, ident[:])
+
+        kind_raw = planes("kind_raw", F32, S)[:3]
+
+        def g1(t):
+            nc.vector.tensor_copy(kind_raw[t][:], tab_win[t][:].indirect(l1[:]))
+
+        for t in range(3):
+            g1(t)
 
         x_pair = mx_pair("x", S)
         nc.vector.tensor_copy(x_pair[0][:], xw[:].bitcast(U32).indirect(l0[:]))
@@ -95,42 +108,33 @@ def tile_picked_tiepathbkinddkindg_none_p_kernel(tc, x_words, x_scales, w1, tab,
 
         w1_bf = keep.tile([P, PACK * H], BF16, name="w1_bf", align_bytes=64)
         nc.scalar.copy(dealt(w1_bf, 0, P // 2), dealing(w1_raw[0][:]))
-        nc.vector.tensor_copy(dealt(w1_bf, P // 2, P), dealing(w1_raw[1][:]))
+        nc.vector.tensor_copy(dealt(w1_bf, P // 2, 3 * P // 4), dealing(w1_raw[1][:, :, : half // 2]))
+        nc.scalar.copy(dealt(w1_bf, 3 * P // 4, P), dealing(w1_raw[1][:, :, half // 2 :]))
         w1_pair = mx_pair("w1", H)
-        for h in range(2):
-            quantize(w1_pair, w1_bf, h * half, (h + 1) * half)
+        for lo, hi in ((0, P), (P, 2 * P), (2 * P, H)):
+            quantize(w1_pair, w1_bf, lo, hi)
+        kind_raw.append(keep.tile([P, S], F32, name="w1_bf", align_bytes=64))
+        g1(3)
 
         size = keep.tile([P, PACK], F32, name="size")
-        size2 = keep.tile([P, PACK], F32, name="size2")
+        minus1 = keep.tile([P, PACK], F32, name="minus1")
+        minus2 = keep.tile([P, PACK], F32, name="minus2")
         step = keep.tile([P, PACK], F32, name="step")
         sgn = keep.tile([P, PACK], F32, name="sgn")
         nc.scalar.activation(size[:], gain[:], ACT.Abs)
-        nc.scalar.activation(size2[:], gain[:], ACT.Abs, scale=2.0)
+        nc.scalar.activation(minus1[:], size[:], ACT.Copy, scale=-1.0)
+        nc.scalar.activation(minus2[:], size[:], ACT.Copy, scale=-2.0)
         nc.gpsimd.tensor_scalar(step[:], gain[:], 0.0, 2.0, ALU.is_ge, ALU.mult)
         nc.gpsimd.tensor_scalar(sgn[:], step[:], 1.0, -1.0, ALU.mult, ALU.add)
 
+        def bank_of(name):
+            return psum.tile([P, S], F32, name=name)
+
+        y_bank = []
         for t in range(PACK):
-            bank = psum.tile([P, S], F32, name="first%d" % t)
+            bank = bank_of("f%d" % t)
             product(bank, w1_pair, t, x_pair)
-            nc.scalar.activation(tab_win[t][:, :S], tab_win[t][:, S:], ACT.Copy, scale=size[:, t : t + 1])
-            nc.scalar.activation(y_win[t][:, :S], bank[:], ACT.Copy, scale=size[:, t : t + 1])
-            nc.scalar.activation(y_win[t][:, S:], bank[:], ACT.Copy, scale=size2[:, t : t + 1])
-
-        s4 = keep.tile([P, PACK, S], F32, name="s4", align_bytes=64)
-        q4 = keep.tile([P, PACK, S], F32, name="q4", align_bytes=64)
-        prod = planes("prod", F32, S)
-
-        def g1(t):
-            nc.vector.tensor_tensor(tab2_win[t][:, S:], tab_win[t][:].indirect(l1[:]), y_win[t][:, :S], ALU.subtract)
-
-        def g2(t):
-            nc.vector.tensor_tensor(s4[:, t, :], y_win[t][:].indirect(l2[:]), tab2_win[t][:, S:], ALU.add)
-
-        def g3(t):
-            nc.vector.tensor_tensor(prod[t][:], tab2_win[t][:].indirect(l3[:]), y_win[t][:, S:], ALU.mult)
-
-        def g4(t):
-            nc.vector.tensor_tensor(q4[:, t, :], y_win[t][:].indirect(l4[:]), prod[t][:], ALU.subtract)
+            y_bank.append(bank)
 
         def skewed(first, second):
             first(0)
@@ -139,57 +143,141 @@ def tile_picked_tiepathbkinddkindg_none_p_kernel(tc, x_words, x_scales, w1, tab,
                 second(t - 1)
             second(PACK - 1)
 
-        def weave(dst, src, func, scale):
-            nc.scalar.activation(dst[:].rearrange("p (c i t) -> p c t i", i=4, t=PACK), src[:].rearrange("p t (c i) -> p c t i", i=4), func, scale=scale)
+        y_twice = planes("y_twice", F32, S)
+        skewed(lambda t: nc.scalar.activation(y_twice[t][:], y_bank[t][:], ACT.Copy, scale=minus2[:, t : t + 1]),
+               lambda t: nc.scalar.activation(y_win[t][:, :S], y_bank[t][:], ACT.Copy, scale=size[:, t : t + 1]))
+        kind = planes("kind", F32, S)[:3] + [keep.tile([P, S], F32, name="w1_codes", align_bytes=64)]
+        for t in range(PACK):
+            nc.scalar.activation(kind[t][:], kind_raw[t][:], ACT.Copy, scale=minus1[:, t : t + 1])
 
-        skewed(g1, g2)
+        def turn(bank, sources, first, last):
+            for k, src in enumerate(sources):
+                for c in range(PACK):
+                    cols = slice(c * P, (c + 1) * P)
+                    nc.tensor.matmul(bank[:, cols], src[:, cols], ident[:], is_transpose=True,
+                                     start=(first and k == 0 and c == 0), stop=(last and k == len(sources) - 1 and c == PACK - 1))
 
-        w2_signed = keep.tile([P, PACK, H], BF16, name="w2_signed", align_bytes=64)
+        diff_bank = [bank_of("f%d" % t) for t in range(PACK)]
+        for t in range(PACK):
+            turn(diff_bank[t], [y_win[t][:, :S], kind[t][:]], True, False)
+
+        q4 = keep.tile([P, PACK, S], F32, name="q4", align_bytes=64)
+        prod = planes("prod", F32, S)
+
+        def g3(t):
+            nc.vector.tensor_tensor(prod[t][:], tab2_win[t][:].indirect(l3[:]), y_twice[t][:], ALU.mult)
+
+        def g4(t):
+            nc.vector.tensor_tensor(q4[:, t, :], y_win[t][:].indirect(l4[:]), prod[t][:], ALU.add)
+
+        skewed(g3, g4)
+
+        shared2 = keep.tile([P, 2 * S], F32, name="shared2", align_bytes=64)
+        z2_bf = shared2[:].bitcast(BF16)
+        w2_signed = z2_bf.rearrange("p (j c) -> p j c", j=PACK)
         for j in range(PACK):
             nc.scalar.activation(w2_signed[:, j, :], w2_raw[:, j, :], ACT.Copy, scale=sgn[:, j : j + 1])
         w2_bf = keep.tile([P, PACK * H], BF16, name="w2_bf", align_bytes=64)
-        nc.scalar.copy(dealt(w2_bf, 0, P), dealing(w2_signed[:]))
+        nc.scalar.copy(dealt(w2_bf, 0, P), dealing(w2_signed))
         w2_pair = mx_pair("w2", H)
         quantize(w2_pair, w2_bf, 0, H)
 
-        z_bf = keep.tile([P, PACK * S], BF16, name="z_bf", align_bytes=64)
-        weave(z_bf, s4, ACT.Abs, 1.0)
-        for t in range(PACK):
-            g3(t)
-        z_pair = mx_pair("z", S)
-        quantize(z_pair, z_bf, 0, S)
-        for t in range(PACK):
-            bank = psum.tile([P, S], F32, name="second%d" % t)
-            product(bank, w2_pair, t, z_pair)
-            nc.scalar.copy(tab_win[t][:, :S], bank[:])
-        for t in range(PACK):
-            g4(t)
-        z2_bf = keep.tile([P, PACK * S], BF16, name="z2_bf", align_bytes=64)
-        weave(z2_bf, q4, ACT.Copy, -0.5)
+        nc.scalar.activation(z2_bf.rearrange("p (c i t) -> p c t i", i=4, t=PACK), q4[:].rearrange("p t (c i) -> p c t i", i=4), ACT.Copy, scale=-0.5)
 
-        a5 = planes("a5_", F32, S)
-        a6 = planes("a6_", F32, S)
-        for t in range(PACK):
-            nc.vector.tensor_copy(a5[t][:], tab_win[t][:].indirect(l5[:]))
+        moved = [y_twice[3][:], prod[2][:], prod[3][:], shared2[:, :S]]
+        diff_t = [q4[:, t, :] for t in range(PACK)]
+
+        def g2(t):
+            nc.vector.tensor_scalar(moved[t], y_win[t][:].indirect(l2[:]), -1.0, 0.0, ALU.mult, ALU.add)
+            turn(diff_bank[t], [moved[t]], False, True)
+
+        def diff(t):
+            nc.scalar.copy(diff_t[t], diff_bank[t][:])
+
+        for t in range(3):
+            g2(t)
+        for t in range(3):
+            diff(t)
         z2_pair = mx_pair("z2", S)
         quantize(z2_pair, z2_bf, 0, S)
         for t in range(PACK):
-            bank = psum.tile([P, S], F32, name="first%d" % t)
+            bank = bank_of("s%d" % t)
             product(bank, w2_pair, t, z2_pair)
             nc.scalar.copy(tab2_win[t][:, :S], bank[:])
+        g2(3)
+        diff(3)
+
+        shared1 = keep.tile([P, 2 * S], F32, name="shared1", align_bytes=64)
+        z_bf = shared1[:].bitcast(BF16)
+        back = [bank_of(name) for name in ("f0", "f1", "s2", "s3")]
         for t in range(PACK):
-            nc.vector.tensor_copy(a6[t][:], tab_win[t][:].indirect(l6[:]))
+            for c in range(PACK):
+                nc.tensor.transpose(back[c][:, t * P : (t + 1) * P], diff_t[t][:, c * P : (c + 1) * P], ident[:])
+        for c in range(PACK):
+            nc.scalar.activation(z_bf[:, c * S : (c + 1) * S].rearrange("p (n t) -> p n t", t=PACK), back[c][:].rearrange("p (t n) -> p n t", t=PACK), ACT.Abs)
 
-        left = planes("left", F32, S)
-        right = planes("right", F32, S)
+        LAST = 2
+        first = planes("first", F32, S)
+        second = [m[:] for m in planes("second", F32, S)[:2]] + [shared1[:, :S], shared1[:, S:]]
+        for t in range(PACK):
+            nc.vector.tensor_copy(first[t][:], tab2_win[t][:].indirect(l7[:]))
+
+        def g8(t):
+            if t < LAST:
+                nc.vector.tensor_tensor(second[t], tab2_win[t][:].indirect(l8[:]), first[t][:], ALU.subtract)
+            else:
+                nc.vector.tensor_copy(second[t], tab2_win[t][:].indirect(l8[:]))
+
+        g8(0)
+        g8(1)
+        u_bank = [bank_of(name) for name in ("f0", "f1")]
+        for t in range(2):
+            turn(u_bank[t], [first[t][:], second[t]], True, False)
+        z_pair = mx_pair("z", S)
+        quantize(z_pair, z_bf, 0, S)
+        for t in range(PACK):
+            bank = bank_of("s%d" % (t % 2))
+            product(bank, w2_pair, t, z_pair)
+            nc.scalar.copy(tab_win[t][:, :S], bank[:])
+        g8(2)
+        g8(3)
+
+        third = planes("third", F32, S)
+        fourth = planes("fourth", F32, S)
+        left_t = planes("left_t", F32, S)
+        rise_t = planes("rise_t", F32, S)
         best = planes("best", F32, S)
+        o_bank = []
 
-        def sums(t):
-            nc.vector.tensor_tensor(left[t][:], tab2_win[t][:].indirect(l7[:]), a5[t][:], ALU.add)
-            nc.vector.tensor_tensor(right[t][:], tab2_win[t][:].indirect(l8[:]), a6[t][:], ALU.add)
+        def g5(t):
+            if t < LAST:
+                nc.vector.tensor_tensor(third[t][:], tab_win[t][:].indirect(l5[:]), second[t], ALU.subtract)
+                turn(u_bank[t], [third[t][:]], False, True)
+                nc.scalar.copy(left_t[t][:], u_bank[t][:])
+                o_bank.append(bank_of(("s2", "s3")[t]))
+                turn(o_bank[t], [left_t[t][:]], True, False)
+            else:
+                nc.vector.tensor_tensor(third[t][:], tab_win[t][:].indirect(l5[:]), first[t][:], ALU.add)
 
-        def larger(t):
-            nc.vector.tensor_tensor(best[t][:], left[t][:], right[t][:], ALU.max)
-            nc.sync.dma_start(by_row(out)[:, t, :], best[t][:])
+        def g6(t):
+            if t < LAST:
+                nc.vector.tensor_tensor(fourth[t][:], tab_win[t][:].indirect(l6[:]), third[t][:], ALU.subtract)
+                d_bank = bank_of("f2")
+                turn(d_bank, [fourth[t][:]], True, True)
+                nc.scalar.activation(rise_t[t][:], d_bank[:], ACT.Relu)
+                turn(o_bank[t], [rise_t[t][:]], False, True)
+                nc.scalar.copy(best[t][:], o_bank[t][:])
+                nc.scalar.dma_start(by_row(out)[:, t, :], best[t][:])
 
-        skewed(sums, larger)
+        for step_fn, t in [(g5, 0), (g5, 1), (g6, 0), (g6, 1), (g5, 2)]:
+            step_fn(t)
+        nc.vector.tensor_tensor(fourth[2][:], tab_win[2][:].indirect(l6[:]), second[2], ALU.add)
+        g5(3)
+        nc.vector.tensor_tensor(best[2][:], third[2][:], fourth[2][:], ALU.max)
+        nc.sync.dma_start(by_row(out)[:, 2, :], best[2][:])
+        halves = [slice(0, S // 2), slice(S // 2, S)]
+        for h, cols in enumerate(halves):
+            nc.vector.tensor_tensor(fourth[3][:, cols], tab_win[3][:].indirect(l6[:, h * 16 : (h + 1) * 16]), second[3][:, cols], ALU.add)
+        for cols in halves:
+            nc.vector.tensor_tensor(best[3][:, cols], third[3][:, cols], fourth[3][:, cols], ALU.max)
+            nc.sync.dma_start(by_row(out)[:, 3, cols], best[3][:, cols])

@@ -18,27 +18,37 @@ PACK = 4
 T = 2048
 S = 512
 H = 512
-FLOPS = 3 * 2 * 512 * 512 * 512
+LIST_COLS = S // 16
+EARLY = 3
+TURNED = 2
+FLOPS = 3 * 2 * H * H * S
 
 
 def tile_picked_tiepathbkinddkindg_none_p_kernel(tc, x_words, x_scales, w1, tab, tab2, gn, w2, offs, n1, n2, n3, n4, n5, n6, n7, n8, out):
     nc = tc.nc
+    last = PACK - 1
     with ExitStack() as ctx:
         lists = ctx.enter_context(tc.tile_pool(name="lists", bufs=1))
         keep = ctx.enter_context(tc.tile_pool(name="keep", bufs=1))
         psum = ctx.enter_context(tc.psum_pool(name="psum", bufs=1))
 
         def load_list(src, name):
-            tile = lists.tile([P, S // 16], U16, name=name)
+            tile = lists.tile([P, LIST_COLS], U16, name=name)
             nc.sync.dma_start(tile[:], src)
             return tile
 
-        def planes(name, dtype, width):
-            return [keep.tile([P, width], dtype, name="%s%d" % (name, t), align_bytes=64) for t in range(PACK)]
+        def planes(name, count, width=S):
+            return [keep.tile([P, width], F32, name="%s%d" % (name, t), align_bytes=64) for t in range(count)]
 
-        def mx_pair(name, width):
-            codes = keep.tile([P, width], U32, name=name + "_codes", align_bytes=64)
-            scales = keep.tile([P, width], U8, name=name + "_scales", align_bytes=64)
+        def bank_of(name):
+            return psum.tile([P, S], F32, name=name)
+
+        def by_row(src):
+            return src.rearrange("(p t) c -> p t c", t=PACK)
+
+        def mx_pair(name):
+            codes = keep.tile([P, S], U32, name=name + "_codes", align_bytes=64)
+            scales = keep.tile([P, S], U8, name=name + "_scales", align_bytes=64)
             return codes, scales
 
         def quantize(pair, src, lo, hi):
@@ -49,30 +59,48 @@ def tile_picked_tiepathbkinddkindg_none_p_kernel(tc, x_words, x_scales, w1, tab,
             nc.tensor.matmul_mx(out=bank[:], lhsT=w_pair[0][:, cols].bitcast(FP8X4), lhsT_scale=w_pair[1][:, cols],
                                 rhs=x_pair[0][:].bitcast(FP8X4), rhs_scale=x_pair[1][:], start=True, stop=True)
 
-        def by_row(src):
-            return src.rearrange("(p t) c -> p t c", t=PACK)
+        def turn(bank, sources, opens, closes):
+            for k, src in enumerate(sources):
+                for c in range(PACK):
+                    cols = slice(c * P, (c + 1) * P)
+                    nc.tensor.matmul(bank[:, cols], src[:, cols], ident[:], is_transpose=True, start=(opens and k == 0 and c == 0),
+                                     stop=(closes and k == len(sources) - 1 and c == last))
 
-        tab_win = planes("tab_win", F32, 2 * S)
-        tab2_win = planes("tab2_win", F32, 2 * S)
-        y_win = planes("y_win", F32, 2 * S)
+        def dealt(dst, lo, hi):
+            return dst[:].rearrange("p (t m j) -> p m t j", t=PACK, j=PACK)[:, lo:hi]
+
+        def dealing(src):
+            return src.rearrange("p j (m t) -> p m t j", t=PACK)
+
+        def skewed(lead, follow):
+            lead(0)
+            for t in range(1, PACK):
+                lead(t)
+                follow(t - 1)
+            follow(last)
+
+        tab_win = planes("tab_win", PACK, 2 * S)
+        tab2_win = planes("tab2_win", PACK, 2 * S)
+        y_win = planes("y_win", PACK, 2 * S)
+
         xw = keep.tile([P, T], I32, name="xw", align_bytes=64)
         xs = keep.tile([P, T], U8, name="xs", align_bytes=64)
         nc.vector.memset(xs[:].bitcast(I32), 0)
         l1 = load_list(n1, "l1")
-        for t in range(2):
+        for t in range(EARLY - 1):
             nc.sync.dma_start(tab_win[t][:, :S], by_row(tab)[:, t, :])
         gain = keep.tile([P, PACK], F32, name="gain")
         nc.sync.dma_start(gain[:], gn.rearrange("(p t) o -> p (t o)", t=PACK))
-        nc.sync.dma_start(tab_win[2][:, :S], by_row(tab)[:, 2, :])
+        nc.sync.dma_start(tab_win[EARLY - 1][:, :S], by_row(tab)[:, EARLY - 1, :])
         nc.sync.dma_start(xw[:], x_words[0].rearrange("p n r -> p (n r)").bitcast(I32))
-        for q in range(4):
-            nc.sync.dma_start(xs[32 * q : 32 * q + 4, :].bitcast(I32), x_scales[0, 4 * q : 4 * q + 4, :].bitcast(I32))
+        for r in range(4):
+            nc.sync.dma_start(xs[r:P:32, :].bitcast(I32), x_scales[0, r:16:4, :].bitcast(I32))
         l0 = load_list(offs, "l0")
         half = H // 2
         w1_raw = [keep.tile([P, PACK, half], F32, name="w1_raw%d" % h, align_bytes=64) for h in range(2)]
         for h in range(2):
             nc.sync.dma_start(w1_raw[h][:], by_row(w1)[:, :, h * half : (h + 1) * half])
-        nc.sync.dma_start(tab_win[3][:, :S], by_row(tab)[:, 3, :])
+        nc.sync.dma_start(tab_win[last][:, S:], by_row(tab)[:, last, :])
         l3 = load_list(n3, "l3")
         l4 = load_list(n4, "l4")
         for t in range(PACK):
@@ -88,196 +116,150 @@ def tile_picked_tiepathbkinddkindg_none_p_kernel(tc, x_words, x_scales, w1, tab,
         ident = keep.tile([P, P], F32, name="ident")
         make_identity(nc, ident[:])
 
-        kind_raw = planes("kind_raw", F32, S)[:3]
-
-        def g1(t):
+        kind_raw = planes("kind_raw", EARLY)
+        for t in range(EARLY):
             nc.vector.tensor_copy(kind_raw[t][:], tab_win[t][:].indirect(l1[:]))
-
-        for t in range(3):
-            g1(t)
-
-        x_pair = mx_pair("x", S)
+        x_pair = mx_pair("x")
         nc.vector.tensor_copy(x_pair[0][:], xw[:].bitcast(U32).indirect(l0[:]))
         nc.vector.tensor_copy(x_pair[1][:], xs[:].indirect(l0[:]))
-
-        def dealt(dst, lo, hi):
-            return dst[:].rearrange("p (t m j) -> p m t j", t=PACK, j=PACK)[:, lo:hi]
-
-        def dealing(src):
-            return src.rearrange("p j (m t) -> p m t j", t=PACK)
 
         w1_bf = keep.tile([P, PACK * H], BF16, name="w1_bf", align_bytes=64)
         nc.scalar.copy(dealt(w1_bf, 0, P // 2), dealing(w1_raw[0][:]))
         nc.vector.tensor_copy(dealt(w1_bf, P // 2, 3 * P // 4), dealing(w1_raw[1][:, :, : half // 2]))
         nc.scalar.copy(dealt(w1_bf, 3 * P // 4, P), dealing(w1_raw[1][:, :, half // 2 :]))
-        w1_pair = mx_pair("w1", H)
+        w1_pair = mx_pair("w1")
         for lo, hi in ((0, P), (P, 2 * P), (2 * P, H)):
             quantize(w1_pair, w1_bf, lo, hi)
-        kind_raw.append(keep.tile([P, S], F32, name="w1_bf", align_bytes=64))
-        g1(3)
 
         size = keep.tile([P, PACK], F32, name="size")
-        minus1 = keep.tile([P, PACK], F32, name="minus1")
         minus2 = keep.tile([P, PACK], F32, name="minus2")
         step = keep.tile([P, PACK], F32, name="step")
         sgn = keep.tile([P, PACK], F32, name="sgn")
         nc.scalar.activation(size[:], gain[:], ACT.Abs)
-        nc.scalar.activation(minus1[:], size[:], ACT.Copy, scale=-1.0)
         nc.scalar.activation(minus2[:], size[:], ACT.Copy, scale=-2.0)
         nc.gpsimd.tensor_scalar(step[:], gain[:], 0.0, 2.0, ALU.is_ge, ALU.mult)
         nc.gpsimd.tensor_scalar(sgn[:], step[:], 1.0, -1.0, ALU.mult, ALU.add)
 
-        def bank_of(name):
-            return psum.tile([P, S], F32, name=name)
+        nc.scalar.activation(tab_win[last][:, :S], tab_win[last][:, S:], ACT.Copy, scale=size[:, last:PACK])
+        kind = planes("kind", EARLY) + [keep.tile([P, S], F32, name="w1_bf", align_bytes=64)]
+        nc.vector.tensor_copy(kind[last][:], tab_win[last][:].indirect(l1[:]))
 
-        y_bank = []
+        y_bank = [bank_of("f%d" % t) for t in range(PACK)]
         for t in range(PACK):
-            bank = bank_of("f%d" % t)
-            product(bank, w1_pair, t, x_pair)
-            y_bank.append(bank)
-
-        def skewed(first, second):
-            first(0)
-            for t in range(1, PACK):
-                first(t)
-                second(t - 1)
-            second(PACK - 1)
-
-        y_twice = planes("y_twice", F32, S)
+            product(y_bank[t], w1_pair, t, x_pair)
+        y_twice = planes("y_twice", PACK)
         skewed(lambda t: nc.scalar.activation(y_twice[t][:], y_bank[t][:], ACT.Copy, scale=minus2[:, t : t + 1]),
                lambda t: nc.scalar.activation(y_win[t][:, :S], y_bank[t][:], ACT.Copy, scale=size[:, t : t + 1]))
-        kind = planes("kind", F32, S)[:3] + [keep.tile([P, S], F32, name="w1_codes", align_bytes=64)]
-        for t in range(PACK):
-            nc.scalar.activation(kind[t][:], kind_raw[t][:], ACT.Copy, scale=minus1[:, t : t + 1])
-
-        def turn(bank, sources, first, last):
-            for k, src in enumerate(sources):
-                for c in range(PACK):
-                    cols = slice(c * P, (c + 1) * P)
-                    nc.tensor.matmul(bank[:, cols], src[:, cols], ident[:], is_transpose=True,
-                                     start=(first and k == 0 and c == 0), stop=(last and k == len(sources) - 1 and c == PACK - 1))
+        for t in range(EARLY):
+            nc.scalar.activation(kind[t][:], kind_raw[t][:], ACT.Copy, scale=size[:, t : t + 1])
 
         diff_bank = [bank_of("f%d" % t) for t in range(PACK)]
         for t in range(PACK):
             turn(diff_bank[t], [y_win[t][:, :S], kind[t][:]], True, False)
 
         q4 = keep.tile([P, PACK, S], F32, name="q4", align_bytes=64)
-        prod = planes("prod", F32, S)
+        prod = planes("prod", PACK)
+        skewed(lambda t: nc.vector.tensor_tensor(prod[t][:], tab2_win[t][:].indirect(l3[:]), y_twice[t][:], ALU.mult),
+               lambda t: nc.vector.tensor_tensor(q4[:, t, :], y_win[t][:].indirect(l4[:]), prod[t][:], ALU.add))
 
-        def g3(t):
-            nc.vector.tensor_tensor(prod[t][:], tab2_win[t][:].indirect(l3[:]), y_twice[t][:], ALU.mult)
-
-        def g4(t):
-            nc.vector.tensor_tensor(q4[:, t, :], y_win[t][:].indirect(l4[:]), prod[t][:], ALU.add)
-
-        skewed(g3, g4)
-
-        shared2 = keep.tile([P, 2 * S], F32, name="shared2", align_bytes=64)
-        z2_bf = shared2[:].bitcast(BF16)
+        z2_bytes = keep.tile([P, 2 * S], F32, name="z2_bytes", align_bytes=64)
+        z2_bf = z2_bytes[:].bitcast(BF16)
         w2_signed = z2_bf.rearrange("p (j c) -> p j c", j=PACK)
         for j in range(PACK):
             nc.scalar.activation(w2_signed[:, j, :], w2_raw[:, j, :], ACT.Copy, scale=sgn[:, j : j + 1])
         w2_bf = keep.tile([P, PACK * H], BF16, name="w2_bf", align_bytes=64)
         nc.scalar.copy(dealt(w2_bf, 0, P), dealing(w2_signed))
-        w2_pair = mx_pair("w2", H)
+        w2_pair = mx_pair("w2")
         quantize(w2_pair, w2_bf, 0, H)
 
-        nc.scalar.activation(z2_bf.rearrange("p (c i t) -> p c t i", i=4, t=PACK), q4[:].rearrange("p t (c i) -> p c t i", i=4), ACT.Copy, scale=-0.5)
+        nc.scalar.activation(z2_bf.rearrange("p (n t) -> p n t", t=PACK), q4[:].rearrange("p t n -> p n t"), ACT.Copy, scale=-0.5)
 
-        moved = [y_twice[3][:], prod[2][:], prod[3][:], shared2[:, :S]]
-        diff_t = [q4[:, t, :] for t in range(PACK)]
+        moved = [tab2_win[last][:, S:], prod[last][:], z2_bytes[:, :S], z2_bytes[:, S:]]
 
-        def g2(t):
-            nc.vector.tensor_scalar(moved[t], y_win[t][:].indirect(l2[:]), -1.0, 0.0, ALU.mult, ALU.add)
+        def close_diff(t):
+            nc.vector.tensor_tensor(moved[t], y_win[t][:].indirect(l2[:]), y_twice[t][:], ALU.add)
             turn(diff_bank[t], [moved[t]], False, True)
 
-        def diff(t):
-            nc.scalar.copy(diff_t[t], diff_bank[t][:])
+        def copy_diff(t):
+            nc.scalar.copy(q4[:, t, :], diff_bank[t][:])
 
-        for t in range(3):
-            g2(t)
-        for t in range(3):
-            diff(t)
-        z2_pair = mx_pair("z2", S)
+        for t in range(2):
+            close_diff(t)
+        for t in range(2):
+            copy_diff(t)
+        z2_pair = mx_pair("z2")
         quantize(z2_pair, z2_bf, 0, S)
         for t in range(PACK):
             bank = bank_of("s%d" % t)
             product(bank, w2_pair, t, z2_pair)
             nc.scalar.copy(tab2_win[t][:, :S], bank[:])
-        g2(3)
-        diff(3)
+        for t in range(2, PACK):
+            close_diff(t)
+        for t in range(2, PACK):
+            copy_diff(t)
 
-        shared1 = keep.tile([P, 2 * S], F32, name="shared1", align_bytes=64)
-        z_bf = shared1[:].bitcast(BF16)
-        back = [bank_of(name) for name in ("f0", "f1", "s2", "s3")]
-        for t in range(PACK):
-            for c in range(PACK):
-                nc.tensor.transpose(back[c][:, t * P : (t + 1) * P], diff_t[t][:, c * P : (c + 1) * P], ident[:])
+        z_bytes = keep.tile([P, 2 * S], F32, name="z_bytes", align_bytes=64)
+        z_bf = z_bytes[:].bitcast(BF16)
         for c in range(PACK):
-            nc.scalar.activation(z_bf[:, c * S : (c + 1) * S].rearrange("p (n t) -> p n t", t=PACK), back[c][:].rearrange("p (t n) -> p n t", t=PACK), ACT.Abs)
+            back = bank_of("s%d" % c)
+            for t in range(PACK):
+                nc.tensor.transpose(back[:, t * P : (t + 1) * P], q4[:, t, c * P : (c + 1) * P], ident[:])
+            nc.scalar.activation(z_bf[:, c * S : (c + 1) * S].rearrange("p (n t) -> p n t", t=PACK), back[:].rearrange("p (t n) -> p n t", t=PACK), ACT.Abs)
 
-        LAST = 2
-        first = planes("first", F32, S)
-        second = [m[:] for m in planes("second", F32, S)[:2]] + [shared1[:, :S], shared1[:, S:]]
+        b7 = planes("b7_", PACK)
+        b8 = [tile[:] for tile in planes("b8_", TURNED)] + [z_bytes[:, :S], z_bytes[:, S:]]
         for t in range(PACK):
-            nc.vector.tensor_copy(first[t][:], tab2_win[t][:].indirect(l7[:]))
-
-        def g8(t):
-            if t < LAST:
-                nc.vector.tensor_tensor(second[t], tab2_win[t][:].indirect(l8[:]), first[t][:], ALU.subtract)
-            else:
-                nc.vector.tensor_copy(second[t], tab2_win[t][:].indirect(l8[:]))
-
-        g8(0)
-        g8(1)
-        u_bank = [bank_of(name) for name in ("f0", "f1")]
-        for t in range(2):
-            turn(u_bank[t], [first[t][:], second[t]], True, False)
-        z_pair = mx_pair("z", S)
+            nc.vector.tensor_copy(b7[t][:], tab2_win[t][:].indirect(l7[:]))
+        for t in range(TURNED):
+            nc.vector.tensor_tensor(b8[t], tab2_win[t][:].indirect(l8[:]), b7[t][:], ALU.subtract)
+        u_bank = [bank_of("s%d" % t) for t in range(TURNED)]
+        for t in range(TURNED):
+            turn(u_bank[t], [b7[t][:], b8[t]], True, False)
+        z_pair = mx_pair("z")
         quantize(z_pair, z_bf, 0, S)
         for t in range(PACK):
-            bank = bank_of("s%d" % (t % 2))
+            bank = bank_of("f%d" % t)
             product(bank, w2_pair, t, z_pair)
             nc.scalar.copy(tab_win[t][:, :S], bank[:])
-        g8(2)
-        g8(3)
+        for t in range(TURNED, PACK):
+            nc.vector.tensor_copy(b8[t], tab2_win[t][:].indirect(l8[:]))
 
-        third = planes("third", F32, S)
-        fourth = planes("fourth", F32, S)
-        left_t = planes("left_t", F32, S)
-        rise_t = planes("rise_t", F32, S)
-        best = planes("best", F32, S)
-        o_bank = []
+        with5 = planes("with5_", PACK)
+        with6 = planes("with6_", PACK)
+        u_turned = planes("u_turned", TURNED)
+        rise_turned = planes("rise_turned", TURNED)
+        best = planes("best", PACK)
+        for t in range(TURNED):
+            nc.vector.tensor_tensor(with5[t][:], tab_win[t][:].indirect(l5[:]), b8[t], ALU.subtract)
+            turn(u_bank[t], [with5[t][:]], False, True)
+            nc.scalar.copy(u_turned[t][:], u_bank[t][:])
+        out_bank = [bank_of("s%d" % (TURNED + t)) for t in range(TURNED)]
+        for t in range(TURNED):
+            nc.vector.tensor_tensor(with6[t][:], tab_win[t][:].indirect(l6[:]), with5[t][:], ALU.subtract)
+            turn(out_bank[t], [u_turned[t][:]], True, False)
+            rise_bank = bank_of("f%d" % (TURNED + t))
+            turn(rise_bank, [with6[t][:]], True, True)
+            nc.scalar.activation(rise_turned[t][:], rise_bank[:], ACT.Relu)
+        for t in range(TURNED):
+            turn(out_bank[t], [rise_turned[t][:]], False, True)
+            nc.scalar.copy(best[t][:], out_bank[t][:])
+            nc.scalar.dma_start(by_row(out)[:, t, :], best[t][:])
 
-        def g5(t):
-            if t < LAST:
-                nc.vector.tensor_tensor(third[t][:], tab_win[t][:].indirect(l5[:]), second[t], ALU.subtract)
-                turn(u_bank[t], [third[t][:]], False, True)
-                nc.scalar.copy(left_t[t][:], u_bank[t][:])
-                o_bank.append(bank_of(("s2", "s3")[t]))
-                turn(o_bank[t], [left_t[t][:]], True, False)
-            else:
-                nc.vector.tensor_tensor(third[t][:], tab_win[t][:].indirect(l5[:]), first[t][:], ALU.add)
+        def make_u(t):
+            nc.vector.tensor_tensor(with5[t][:], tab_win[t][:].indirect(l5[:]), b7[t][:], ALU.add)
 
-        def g6(t):
-            if t < LAST:
-                nc.vector.tensor_tensor(fourth[t][:], tab_win[t][:].indirect(l6[:]), third[t][:], ALU.subtract)
-                d_bank = bank_of("f2")
-                turn(d_bank, [fourth[t][:]], True, True)
-                nc.scalar.activation(rise_t[t][:], d_bank[:], ACT.Relu)
-                turn(o_bank[t], [rise_t[t][:]], False, True)
-                nc.scalar.copy(best[t][:], o_bank[t][:])
-                nc.scalar.dma_start(by_row(out)[:, t, :], best[t][:])
+        def make_v(t, lo, hi):
+            nc.vector.tensor_tensor(with6[t][:, lo:hi], tab_win[t][:].indirect(l6[:, lo // 16 : hi // 16]), b8[t][:, lo:hi], ALU.add)
 
-        for step_fn, t in [(g5, 0), (g5, 1), (g6, 0), (g6, 1), (g5, 2)]:
-            step_fn(t)
-        nc.vector.tensor_tensor(fourth[2][:], tab_win[2][:].indirect(l6[:]), second[2], ALU.add)
-        g5(3)
-        nc.vector.tensor_tensor(best[2][:], third[2][:], fourth[2][:], ALU.max)
-        nc.sync.dma_start(by_row(out)[:, 2, :], best[2][:])
-        halves = [slice(0, S // 2), slice(S // 2, S)]
-        for h, cols in enumerate(halves):
-            nc.vector.tensor_tensor(fourth[3][:, cols], tab_win[3][:].indirect(l6[:, h * 16 : (h + 1) * 16]), second[3][:, cols], ALU.add)
-        for cols in halves:
-            nc.vector.tensor_tensor(best[3][:, cols], third[3][:, cols], fourth[3][:, cols], ALU.max)
-            nc.sync.dma_start(by_row(out)[:, 3, cols], best[3][:, cols])
+        def store_max(t, lo, hi):
+            nc.vector.tensor_tensor(best[t][:, lo:hi], with5[t][:, lo:hi], with6[t][:, lo:hi], ALU.max)
+            nc.sync.dma_start(by_row(out)[:, t, lo:hi], best[t][:, lo:hi])
+
+        make_u(2)
+        make_v(2, 0, S)
+        make_u(last)
+        store_max(2, 0, S)
+        for lo in (0, S // 2):
+            make_v(last, lo, lo + S // 2)
+        for lo in (0, S // 2):
+            store_max(last, lo, lo + S // 2)

from contextlib import ExitStack

import concourse.mybir as mybir
from concourse.masks import make_identity

F32 = mybir.dt.float32
BF16 = mybir.dt.bfloat16
I32 = mybir.dt.int32
U32 = mybir.dt.uint32
U16 = mybir.dt.uint16
U8 = mybir.dt.uint8
FP8X4 = mybir.dt.float8_e4m3fn_x4
ALU = mybir.AluOpType
ACT = mybir.ActivationFunctionType

P = 128
PACK = 4
T = 2048
S = 512
H = 512
LIST_COLS = S // 16
EARLY = 3
TURNED = 2
FLOPS = 3 * 2 * H * H * S


def tile_picked_tiepathbkinddkindg_none_p_kernel(tc, x_words, x_scales, w1, tab, tab2, gn, w2, offs, n1, n2, n3, n4, n5, n6, n7, n8, out):
    nc = tc.nc
    last = PACK - 1
    with ExitStack() as ctx:
        lists = ctx.enter_context(tc.tile_pool(name="lists", bufs=1))
        keep = ctx.enter_context(tc.tile_pool(name="keep", bufs=1))
        psum = ctx.enter_context(tc.psum_pool(name="psum", bufs=1))

        def load_list(src, name):
            tile = lists.tile([P, LIST_COLS], U16, name=name)
            nc.sync.dma_start(tile[:], src)
            return tile

        def planes(name, count, width=S):
            return [keep.tile([P, width], F32, name="%s%d" % (name, t), align_bytes=64) for t in range(count)]

        def bank_of(name):
            return psum.tile([P, S], F32, name=name)

        def by_row(src):
            return src.rearrange("(p t) c -> p t c", t=PACK)

        def mx_pair(name):
            codes = keep.tile([P, S], U32, name=name + "_codes", align_bytes=64)
            scales = keep.tile([P, S], U8, name=name + "_scales", align_bytes=64)
            return codes, scales

        def quantize(pair, src, lo, hi):
            nc.vector.quantize_mx(out=pair[0][:, lo:hi].bitcast(FP8X4), scales=pair[1][:, lo:hi], in_=src[:, PACK * lo : PACK * hi])

        def product(bank, w_pair, t, x_pair):
            cols = slice(t * P, (t + 1) * P)
            nc.tensor.matmul_mx(out=bank[:], lhsT=w_pair[0][:, cols].bitcast(FP8X4), lhsT_scale=w_pair[1][:, cols],
                                rhs=x_pair[0][:].bitcast(FP8X4), rhs_scale=x_pair[1][:], start=True, stop=True)

        def turn(bank, sources, opens, closes):
            for k, src in enumerate(sources):
                for c in range(PACK):
                    cols = slice(c * P, (c + 1) * P)
                    nc.tensor.matmul(bank[:, cols], src[:, cols], ident[:], is_transpose=True, start=(opens and k == 0 and c == 0),
                                     stop=(closes and k == len(sources) - 1 and c == last))

        def dealt(dst, lo, hi):
            return dst[:].rearrange("p (t m j) -> p m t j", t=PACK, j=PACK)[:, lo:hi]

        def dealing(src):
            return src.rearrange("p j (m t) -> p m t j", t=PACK)

        def skewed(lead, follow):
            lead(0)
            for t in range(1, PACK):
                lead(t)
                follow(t - 1)
            follow(last)

        tab_win = planes("tab_win", PACK, 2 * S)
        tab2_win = planes("tab2_win", PACK, 2 * S)
        y_win = planes("y_win", PACK, 2 * S)

        xw = keep.tile([P, T], I32, name="xw", align_bytes=64)
        xs = keep.tile([P, T], U8, name="xs", align_bytes=64)
        nc.vector.memset(xs[:].bitcast(I32), 0)
        l1 = load_list(n1, "l1")
        for t in range(EARLY - 1):
            nc.sync.dma_start(tab_win[t][:, :S], by_row(tab)[:, t, :])
        gain = keep.tile([P, PACK], F32, name="gain")
        nc.sync.dma_start(gain[:], gn.rearrange("(p t) o -> p (t o)", t=PACK))
        nc.sync.dma_start(tab_win[EARLY - 1][:, :S], by_row(tab)[:, EARLY - 1, :])
        nc.sync.dma_start(xw[:], x_words[0].rearrange("p n r -> p (n r)").bitcast(I32))
        for r in range(4):
            nc.sync.dma_start(xs[r:P:32, :].bitcast(I32), x_scales[0, r:16:4, :].bitcast(I32))
        l0 = load_list(offs, "l0")
        half = H // 2
        w1_raw = [keep.tile([P, PACK, half], F32, name="w1_raw%d" % h, align_bytes=64) for h in range(2)]
        for h in range(2):
            nc.sync.dma_start(w1_raw[h][:], by_row(w1)[:, :, h * half : (h + 1) * half])
        nc.sync.dma_start(tab_win[last][:, S:], by_row(tab)[:, last, :])
        l3 = load_list(n3, "l3")
        l4 = load_list(n4, "l4")
        for t in range(PACK):
            nc.sync.dma_start(tab2_win[t][:, :S], by_row(tab2)[:, t, :])
        w2_raw = keep.tile([P, PACK, H], F32, name="w2_raw", align_bytes=64)
        nc.sync.dma_start(w2_raw[:], by_row(w2))
        l2 = load_list(n2, "l2")
        l7 = load_list(n7, "l7")
        l8 = load_list(n8, "l8")
        l5 = load_list(n5, "l5")
        l6 = load_list(n6, "l6")

        ident = keep.tile([P, P], F32, name="ident")
        make_identity(nc, ident[:])

        kind_raw = planes("kind_raw", EARLY)
        for t in range(EARLY):
            nc.vector.tensor_copy(kind_raw[t][:], tab_win[t][:].indirect(l1[:]))
        x_pair = mx_pair("x")
        nc.vector.tensor_copy(x_pair[0][:], xw[:].bitcast(U32).indirect(l0[:]))
        nc.vector.tensor_copy(x_pair[1][:], xs[:].indirect(l0[:]))

        w1_bf = keep.tile([P, PACK * H], BF16, name="w1_bf", align_bytes=64)
        nc.scalar.copy(dealt(w1_bf, 0, P // 2), dealing(w1_raw[0][:]))
        nc.vector.tensor_copy(dealt(w1_bf, P // 2, 3 * P // 4), dealing(w1_raw[1][:, :, : half // 2]))
        nc.scalar.copy(dealt(w1_bf, 3 * P // 4, P), dealing(w1_raw[1][:, :, half // 2 :]))
        w1_pair = mx_pair("w1")
        for lo, hi in ((0, P), (P, 2 * P), (2 * P, H)):
            quantize(w1_pair, w1_bf, lo, hi)

        size = keep.tile([P, PACK], F32, name="size")
        minus2 = keep.tile([P, PACK], F32, name="minus2")
        step = keep.tile([P, PACK], F32, name="step")
        sgn = keep.tile([P, PACK], F32, name="sgn")
        nc.scalar.activation(size[:], gain[:], ACT.Abs)
        nc.scalar.activation(minus2[:], size[:], ACT.Copy, scale=-2.0)
        nc.gpsimd.tensor_scalar(step[:], gain[:], 0.0, 2.0, ALU.is_ge, ALU.mult)
        nc.gpsimd.tensor_scalar(sgn[:], step[:], 1.0, -1.0, ALU.mult, ALU.add)

        nc.scalar.activation(tab_win[last][:, :S], tab_win[last][:, S:], ACT.Copy, scale=size[:, last:PACK])
        kind = planes("kind", EARLY) + [keep.tile([P, S], F32, name="w1_bf", align_bytes=64)]
        nc.vector.tensor_copy(kind[last][:], tab_win[last][:].indirect(l1[:]))

        y_bank = [bank_of("f%d" % t) for t in range(PACK)]
        for t in range(PACK):
            product(y_bank[t], w1_pair, t, x_pair)
        y_twice = planes("y_twice", PACK)
        skewed(lambda t: nc.scalar.activation(y_twice[t][:], y_bank[t][:], ACT.Copy, scale=minus2[:, t : t + 1]),
               lambda t: nc.scalar.activation(y_win[t][:, :S], y_bank[t][:], ACT.Copy, scale=size[:, t : t + 1]))
        for t in range(EARLY):
            nc.scalar.activation(kind[t][:], kind_raw[t][:], ACT.Copy, scale=size[:, t : t + 1])

        diff_bank = [bank_of("f%d" % t) for t in range(PACK)]
        for t in range(PACK):
            turn(diff_bank[t], [y_win[t][:, :S], kind[t][:]], True, False)

        q4 = keep.tile([P, PACK, S], F32, name="q4", align_bytes=64)
        prod = planes("prod", PACK)
        skewed(lambda t: nc.vector.tensor_tensor(prod[t][:], tab2_win[t][:].indirect(l3[:]), y_twice[t][:], ALU.mult),
               lambda t: nc.vector.tensor_tensor(q4[:, t, :], y_win[t][:].indirect(l4[:]), prod[t][:], ALU.add))

        z2_bytes = keep.tile([P, 2 * S], F32, name="z2_bytes", align_bytes=64)
        z2_bf = z2_bytes[:].bitcast(BF16)
        w2_signed = z2_bf.rearrange("p (j c) -> p j c", j=PACK)
        for j in range(PACK):
            nc.scalar.activation(w2_signed[:, j, :], w2_raw[:, j, :], ACT.Copy, scale=sgn[:, j : j + 1])
        w2_bf = keep.tile([P, PACK * H], BF16, name="w2_bf", align_bytes=64)
        nc.scalar.copy(dealt(w2_bf, 0, P), dealing(w2_signed))
        w2_pair = mx_pair("w2")
        quantize(w2_pair, w2_bf, 0, H)

        nc.scalar.activation(z2_bf.rearrange("p (n t) -> p n t", t=PACK), q4[:].rearrange("p t n -> p n t"), ACT.Copy, scale=-0.5)

        moved = [tab2_win[last][:, S:], prod[last][:], z2_bytes[:, :S], z2_bytes[:, S:]]

        def close_diff(t):
            nc.vector.tensor_tensor(moved[t], y_win[t][:].indirect(l2[:]), y_twice[t][:], ALU.add)
            turn(diff_bank[t], [moved[t]], False, True)

        def copy_diff(t):
            nc.scalar.copy(q4[:, t, :], diff_bank[t][:])

        for t in range(2):
            close_diff(t)
        for t in range(2):
            copy_diff(t)
        z2_pair = mx_pair("z2")
        quantize(z2_pair, z2_bf, 0, S)
        for t in range(PACK):
            bank = bank_of("s%d" % t)
            product(bank, w2_pair, t, z2_pair)
            nc.scalar.copy(tab2_win[t][:, :S], bank[:])
        for t in range(2, PACK):
            close_diff(t)
        for t in range(2, PACK):
            copy_diff(t)

        z_bytes = keep.tile([P, 2 * S], F32, name="z_bytes", align_bytes=64)
        z_bf = z_bytes[:].bitcast(BF16)
        for c in range(PACK):
            back = bank_of("s%d" % c)
            for t in range(PACK):
                nc.tensor.transpose(back[:, t * P : (t + 1) * P], q4[:, t, c * P : (c + 1) * P], ident[:])
            nc.scalar.activation(z_bf[:, c * S : (c + 1) * S].rearrange("p (n t) -> p n t", t=PACK), back[:].rearrange("p (t n) -> p n t", t=PACK), ACT.Abs)

        b7 = planes("b7_", PACK)
        b8 = [tile[:] for tile in planes("b8_", TURNED)] + [z_bytes[:, :S], z_bytes[:, S:]]
        for t in range(PACK):
            nc.vector.tensor_copy(b7[t][:], tab2_win[t][:].indirect(l7[:]))
        for t in range(TURNED):
            nc.vector.tensor_tensor(b8[t], tab2_win[t][:].indirect(l8[:]), b7[t][:], ALU.subtract)
        u_bank = [bank_of("s%d" % t) for t in range(TURNED)]
        for t in range(TURNED):
            turn(u_bank[t], [b7[t][:], b8[t]], True, False)
        z_pair = mx_pair("z")
        quantize(z_pair, z_bf, 0, S)
        for t in range(PACK):
            bank = bank_of("f%d" % t)
            product(bank, w2_pair, t, z_pair)
            nc.scalar.copy(tab_win[t][:, :S], bank[:])
        for t in range(TURNED, PACK):
            nc.vector.tensor_copy(b8[t], tab2_win[t][:].indirect(l8[:]))

        with5 = planes("with5_", PACK)
        with6 = planes("with6_", PACK)
        u_turned = planes("u_turned", TURNED)
        rise_turned = planes("rise_turned", TURNED)
        best = planes("best", PACK)
        for t in range(TURNED):
            nc.vector.tensor_tensor(with5[t][:], tab_win[t][:].indirect(l5[:]), b8[t], ALU.subtract)
            turn(u_bank[t], [with5[t][:]], False, True)
            nc.scalar.copy(u_turned[t][:], u_bank[t][:])
        out_bank = [bank_of("s%d" % (TURNED + t)) for t in range(TURNED)]
        for t in range(TURNED):
            nc.vector.tensor_tensor(with6[t][:], tab_win[t][:].indirect(l6[:]), with5[t][:], ALU.subtract)
            turn(out_bank[t], [u_turned[t][:]], True, False)
            rise_bank = bank_of("f%d" % (TURNED + t))
            turn(rise_bank, [with6[t][:]], True, True)
            nc.scalar.activation(rise_turned[t][:], rise_bank[:], ACT.Relu)
        for t in range(TURNED):
            turn(out_bank[t], [rise_turned[t][:]], False, True)
            nc.scalar.copy(best[t][:], out_bank[t][:])
            nc.scalar.dma_start(by_row(out)[:, t, :], best[t][:])

        def make_u(t):
            nc.vector.tensor_tensor(with5[t][:], tab_win[t][:].indirect(l5[:]), b7[t][:], ALU.add)

        def make_v(t, lo, hi):
            nc.vector.tensor_tensor(with6[t][:, lo:hi], tab_win[t][:].indirect(l6[:, lo // 16 : hi // 16]), b8[t][:, lo:hi], ALU.add)

        def store_max(t, lo, hi):
            nc.vector.tensor_tensor(best[t][:, lo:hi], with5[t][:, lo:hi], with6[t][:, lo:hi], ALU.max)
            nc.sync.dma_start(by_row(out)[:, t, lo:hi], best[t][:, lo:hi])

        make_u(2)
        make_v(2, 0, S)
        make_u(last)
        store_max(2, 0, S)
        for lo in (0, S // 2):
            make_v(last, lo, lo + S // 2)
        for lo in (0, S // 2):
            store_max(last, lo, lo + S // 2)
